import numpy as np
import ml_dtypes


def mxq(x, axis, fmt="e4m3"):
    dtype, down = {"e4m3": (ml_dtypes.float8_e4m3fn, 7), "e5m2": (ml_dtypes.float8_e5m2, 14)}[fmt]
    v = np.moveaxis(np.asarray(x, np.float32).astype(ml_dtypes.bfloat16).astype(np.float64), axis, -1)
    blocks = v.reshape(v.shape[:-1] + (-1, 32))
    amax = np.abs(blocks).max(-1, keepdims=True)
    byte = np.maximum(np.where(amax > 0, np.frexp(amax)[1] - 1 + 127, 0) - down, 1)
    scale = np.exp2(byte - 127.0)
    codes = (blocks / scale).astype(np.float32).astype(dtype).astype(np.float64)
    return np.moveaxis((codes * scale).reshape(v.shape), -1, axis)


WIDE = False


def mx_kscale(k):
    if not WIDE:
        return np.ones(k)
    levels = np.array([10, -10, 5, -5, 0])
    if k % 512:
        return np.exp2(np.random.permutation(np.resize(levels, k // 32))).repeat(32)
    a = np.empty((k // 512, 16))
    for p in range(k // 512):
        a[p, :8] = np.random.permutation(np.resize(levels, 8))
        for g in range(8):
            far = levels[np.abs(levels - a[p, g]) >= 10]
            a[p, g + 8] = far[np.random.randint(len(far))]
    return np.exp2(a.ravel()).repeat(32)


def f64(x):
    return np.asarray(x).astype(np.float64)


def striped8(idx):
    return np.asarray(idx).reshape(8, -1, 16).transpose(0, 2, 1).reshape(128, -1).astype(np.uint16)


def unstriped8(offs):
    return offs.reshape(8, 16, -1).transpose(0, 2, 1).reshape(8, -1).astype(np.int64)


def pick8(x, idx, run):
    r = np.arange(len(x))
    return x[r[:, None], idx[r % (8 * run) // run]]


E2M1 = np.array([0.0, 0.5, 1.0, 1.5, 2.0, 3.0, 4.0, 6.0, -0.0, -0.5, -1.0, -1.5, -2.0, -3.0, -4.0, -6.0])


def pack_weight(w, fmt):
    k, n = w.shape
    w = f64(np.asarray(w, np.float32).astype(ml_dtypes.bfloat16)).reshape(k // 32, 32, n)
    amax = np.abs(w).max(1)
    if fmt == "e4m3":
        byte = np.frexp(amax)[1] - 1 + 127 - 7
    else:
        mant, ex = np.frexp(amax / 6.0)
        byte = np.where(mant > 0.5, ex, ex - 1) + 127
    byte = np.clip(np.where(amax > 0, byte, 1), 1, 254)
    scaled = (w * np.exp2(127.0 - byte)[:, None, :]).reshape(k, n).astype(np.float32)
    by_word = np.ascontiguousarray(scaled.reshape(k // 512, 128, 4, n).transpose(0, 1, 3, 2))
    if fmt == "e4m3":
        words = by_word.astype(ml_dtypes.float8_e4m3fn).view(np.uint8)
    else:
        c = by_word.astype(ml_dtypes.float4_e2m1fn).view(np.uint8) & 0xF
        words = (c[..., 0::2] | (c[..., 1::2] << 4)).reshape(k // 512, 128, 2 * n)
    return np.ascontiguousarray(words), np.ascontiguousarray(byte.astype(np.uint8).reshape(k // 512, 16, n))


def unpack_weight(words, scales, fmt):
    g, _, n = scales.shape
    words = np.ascontiguousarray(words).reshape(g, 128, n, -1)
    if fmt == "e4m3":
        vals = words.view(ml_dtypes.float8_e4m3fn).astype(np.float64)
    else:
        nib = np.empty((g, 128, n, 4), np.uint8)
        nib[..., 0::2] = words & 0xF
        nib[..., 1::2] = words >> 4
        vals = E2M1[nib]
    vals = vals * np.repeat(np.exp2(scales.astype(np.float64) - 127.0), 8, axis=1)[..., None]
    return vals.transpose(0, 1, 3, 2).reshape(g * 512, n)


D, T, I, Q = 512, 1024, 512, 128


def setup_inputs():
    n = np.random.standard_normal
    idx = np.stack([np.random.permutation(T)[:I] for _ in range(8)])
    idx2 = np.stack([np.random.permutation(T)[:I] for _ in range(8)])
    idx3 = np.stack([np.random.permutation(T)[:I] for _ in range(8)])
    idx4 = np.stack([np.random.permutation(T)[:I] for _ in range(8)])
    fd = mx_kscale(D)
    keysp = pack_weight(n((D, T)) / fd[:, None], "e4m3")
    return {
        "query": (n((D, Q)) * 1.0 / np.sqrt(D) * fd[:, None]).astype(np.float32),
        "keys_words": keysp[0],
        "keys_scales": keysp[1],
        "old": (np.random.uniform(0.3, 1.7, (Q, T))).astype(np.float32),
        "base": (0.5 * n((Q, T))).astype(np.float32),
        "offs": striped8(idx),
        "offs2": striped8(idx2),
        "offs3": striped8(idx3),
        "offs4": striped8(idx4),
    }


def reference(query, keys_words, keys_scales, old, base, offs, offs2, offs3, offs4):
    idx = unstriped8(offs)
    idx2 = unstriped8(offs2)
    idx3 = unstriped8(offs3)
    idx4 = unstriped8(offs4)
    keysu = unpack_weight(keys_words, keys_scales, "e4m3")
    queryq = mxq(f64(query), 0, "e4m3")
    a = queryq.T @ keysu
    w = pick8(a, idx, 16) * pick8(a, idx2, 16)
    ws = w * pick8(f64(old), idx3, 16)
    f1 = np.zeros((Q, T))
    f1[np.arange(Q)[:, None], idx4[np.arange(Q) % 128 // 16]] = ws
    y = f64(base) + f1
    return y

@@ -1,0 +1,121 @@
+from contextlib import ExitStack
+
+import concourse.mybir as mybir
+
+D, T, SLOTS, Q = 512, 1024, 512, 128
+FLOPS = 2 * D * T * Q
+
+F32 = mybir.dt.float32
+BF16 = mybir.dt.bfloat16
+I32 = mybir.dt.int32
+U32 = mybir.dt.uint32
+U16 = mybir.dt.uint16
+U8 = mybir.dt.uint8
+FP8X4 = mybir.dt.float8_e4m3fn_x4
+MULT = mybir.AluOpType.mult
+ADD = mybir.AluOpType.add
+COPY = mybir.ActivationFunctionType.Copy
+
+P = 128
+PACK = 4
+LIST_COLS = SLOTS // 16
+KEY_LOADS = 2
+N_TILE = 256
+HALF = SLOTS // 2
+STORE_COLS = 256
+
+
+def tile_attend_pairproduct_lean_timesold_heads_kernel(
+    tc, query, keys_words, keys_scales, old, base, offs, offs2, offs3, offs4, out
+):
+    nc = tc.nc
+    with ExitStack() as ctx:
+        pool = ctx.enter_context(tc.tile_pool(name="held", bufs=1))
+        psum = ctx.enter_context(tc.psum_pool(name="psum", bufs=1))
+
+        key_scales = pool.tile([P, T], U8, name="key_scales", align_bytes=64)
+        nc.vector.memset(key_scales[:].bitcast(I32), 0)
+        q_raw = pool.tile([P, PACK, Q], F32, name="q_raw")
+        nc.sync.dma_start(out=q_raw[:], in_=query.rearrange("(p j) q -> p j q", j=PACK))
+        for quad in range(4):
+            nc.scalar.dma_start(
+                out=key_scales[32 * quad : 32 * quad + 4, :].bitcast(I32),
+                in_=keys_scales[0, 4 * quad : 4 * quad + 4, :].bitcast(I32),
+            )
+        words_i32 = keys_words[0].rearrange("p t r -> p (t r)").bitcast(I32)
+        load_cols = T // KEY_LOADS
+        key_words = []
+        for h in range(KEY_LOADS):
+            part = pool.tile([P, load_cols], U32, name="key_words%d" % h, align_bytes=64)
+            nc.sync.dma_start(out=part[:].bitcast(I32), in_=words_i32[:, h * load_cols : (h + 1) * load_cols])
+            key_words.append(part)
+        old_sb = pool.tile([P, T], F32, name="old_sb")
+        nc.sync.dma_start(out=old_sb[:], in_=old)
+        list3 = pool.tile([P, LIST_COLS], U16, name="list3")
+        nc.sync.dma_start(list3[:], offs3)
+        list1 = pool.tile([P, LIST_COLS], U16, name="list1")
+        nc.sync.dma_start(list1[:], offs)
+        list2 = pool.tile([P, LIST_COLS], U16, name="list2")
+        nc.sync.dma_start(list2[:], offs2)
+        list4 = pool.tile([P, LIST_COLS], U16, name="list4")
+        nc.sync.dma_start(list4[:], offs4)
+        base_sb = pool.tile([P, T], F32, name="base_sb")
+        nc.sync.dma_start(out=base_sb[:], in_=base)
+
+        placed = pool.tile([P, T], F32, name="placed")
+        nc.vector.memset(placed[:], 0.0)
+
+        q_bf = pool.tile([P, Q, PACK], BF16, name="q_bf", align_bytes=64)
+        nc.vector.tensor_copy(out=q_bf[:], in_=q_raw[:].rearrange("p j q -> p q j"))
+        q_codes = pool.tile([P, Q], U32, name="q_codes", align_bytes=64)
+        q_scales = pool.tile([P, Q], U8, name="q_scales", align_bytes=64)
+        nc.vector.quantize_mx(
+            out=q_codes[:].bitcast(FP8X4), scales=q_scales[:], in_=q_bf[:].rearrange("p q j -> p (q j)")
+        )
+
+        scores = pool.tile([P, T], F32, name="scores")
+        for n in range(T // N_TILE):
+            cols = slice(n * N_TILE, (n + 1) * N_TILE)
+            h, c0 = divmod(n * N_TILE, load_cols)
+            bank = psum.tile([P, N_TILE], F32, name="bank%d" % n)
+            nc.tensor.matmul_mx(
+                out=bank[:],
+                lhsT=q_codes[:].bitcast(FP8X4),
+                lhsT_scale=q_scales[:],
+                rhs=key_words[h][:, c0 : c0 + N_TILE].bitcast(FP8X4),
+                rhs_scale=key_scales[:, cols],
+                start=True,
+                stop=True,
+            )
+            if n % 2 == 0:
+                nc.scalar.activation(scores[:, cols], bank[:], COPY)
+            else:
+                nc.vector.tensor_copy(out=scores[:, cols], in_=bank[:])
+
+        first = slice(0, LIST_COLS // 2)
+        second = slice(LIST_COLS // 2, LIST_COLS)
+
+        old_a = pool.tile([P, HALF], F32, name="old_a")
+        nc.scalar.activation(old_a[:], old_sb[:].indirect(list3[:, first]), COPY)
+        left_a = pool.tile([P, HALF], F32, name="left_a")
+        nc.scalar.activation(left_a[:], scores[:].indirect(list1[:, first]), COPY)
+        right_a = pool.tile([P, HALF], F32, name="right_a")
+        nc.vector.tensor_tensor(right_a[:], scores[:].indirect(list2[:, first]), old_a[:], MULT)
+        nc.vector.tensor_tensor(placed[:].indirect(list4[:, first]), left_a[:], right_a[:], MULT)
+
+        old_b = pool.tile([P, HALF], F32, name="old_b")
+        nc.scalar.activation(old_b[:], old_sb[:].indirect(list3[:, second]), COPY)
+        mid_b = pool.tile([P, HALF], F32, name="mid_b")
+        nc.scalar.activation(mid_b[:], scores[:].indirect(list2[:, second]), COPY)
+        left_b = pool.tile([P, HALF], F32, name="left_b")
+        nc.scalar.activation(left_b[:], scores[:].indirect(list1[:, second]), COPY)
+        right_b = pool.tile([P, HALF], F32, name="right_b")
+        nc.vector.tensor_tensor(right_b[:], mid_b[:], old_b[:], MULT)
+        nc.vector.tensor_tensor(placed[:].indirect(list4[:, second]), left_b[:], right_b[:], MULT)
+
+        for s in range(T // STORE_COLS):
+            cols = slice(s * STORE_COLS, (s + 1) * STORE_COLS)
+            result = pool.tile([P, STORE_COLS], F32, name="result%d" % s)
+            nc.vector.tensor_tensor(result[:], placed[:, cols], base_sb[:, cols], ADD)
+            queue = nc.sync if s % 2 == 0 else nc.scalar
+            queue.dma_start(out=out[:, cols], in_=result[:])

@@ -23,6 +23,7 @@ KEY_LOADS = 2
 N_TILE = 256
 HALF = SLOTS // 2
 STORE_COLS = 256
+Q_SPLIT = 88
 
 
 def tile_attend_pairproduct_lean_timesold_heads_kernel(
@@ -34,13 +35,13 @@ def tile_attend_pairproduct_lean_timesold_heads_kernel(
         psum = ctx.enter_context(tc.psum_pool(name="psum", bufs=1))
 
         key_scales = pool.tile([P, T], U8, name="key_scales", align_bytes=64)
-        nc.vector.memset(key_scales[:].bitcast(I32), 0)
-        q_raw = pool.tile([P, PACK, Q], F32, name="q_raw")
+        q_raw = pool.tile([P, PACK, Q], F32, name="q_raw", tag="q_then_base")
         nc.sync.dma_start(out=q_raw[:], in_=query.rearrange("(p j) q -> p j q", j=PACK))
         for quad in range(4):
-            nc.scalar.dma_start(
-                out=key_scales[32 * quad : 32 * quad + 4, :].bitcast(I32),
-                in_=keys_scales[0, 4 * quad : 4 * quad + 4, :].bitcast(I32),
+            rows = keys_scales[0, 4 * quad : 4 * quad + 4, :].bitcast(I32)
+            nc.sync.dma_start(
+                out=key_scales[32 * quad : 32 * quad + 32, :].bitcast(I32),
+                in_=rows.unsqueeze(0).broadcast_to([8, 4, T // 4]),
             )
         words_i32 = keys_words[0].rearrange("p t r -> p (t r)").bitcast(I32)
         load_cols = T // KEY_LOADS
@@ -49,7 +50,7 @@ def tile_attend_pairproduct_lean_timesold_heads_kernel(
             part = pool.tile([P, load_cols], U32, name="key_words%d" % h, align_bytes=64)
             nc.sync.dma_start(out=part[:].bitcast(I32), in_=words_i32[:, h * load_cols : (h + 1) * load_cols])
             key_words.append(part)
-        old_sb = pool.tile([P, T], F32, name="old_sb")
+        old_sb = pool.tile([P, T], F32, name="old_sb", tag="old_then_second")
         nc.sync.dma_start(out=old_sb[:], in_=old)
         list3 = pool.tile([P, LIST_COLS], U16, name="list3")
         nc.sync.dma_start(list3[:], offs3)
@@ -59,19 +60,22 @@ def tile_attend_pairproduct_lean_timesold_heads_kernel(
         nc.sync.dma_start(list2[:], offs2)
         list4 = pool.tile([P, LIST_COLS], U16, name="list4")
         nc.sync.dma_start(list4[:], offs4)
-        base_sb = pool.tile([P, T], F32, name="base_sb")
-        nc.sync.dma_start(out=base_sb[:], in_=base)
 
         placed = pool.tile([P, T], F32, name="placed")
         nc.vector.memset(placed[:], 0.0)
 
         q_bf = pool.tile([P, Q, PACK], BF16, name="q_bf", align_bytes=64)
-        nc.vector.tensor_copy(out=q_bf[:], in_=q_raw[:].rearrange("p j q -> p q j"))
+        q_view = q_raw[:].rearrange("p j q -> p q j")
+        nc.vector.tensor_copy(out=q_bf[:, :Q_SPLIT, :], in_=q_view[:, :Q_SPLIT, :])
+        nc.scalar.activation(q_bf[:, Q_SPLIT:, :], q_view[:, Q_SPLIT:, :], COPY)
         q_codes = pool.tile([P, Q], U32, name="q_codes", align_bytes=64)
         q_scales = pool.tile([P, Q], U8, name="q_scales", align_bytes=64)
         nc.vector.quantize_mx(
             out=q_codes[:].bitcast(FP8X4), scales=q_scales[:], in_=q_bf[:].rearrange("p q j -> p (q j)")
         )
+
+        base_sb = pool.tile([P, T], F32, name="base_sb", tag="q_then_base")
+        nc.sync.dma_start(out=base_sb[:], in_=base)
 
         scores = pool.tile([P, T], F32, name="scores")
         for n in range(T // N_TILE):
@@ -87,10 +91,7 @@ def tile_attend_pairproduct_lean_timesold_heads_kernel(
                 start=True,
                 stop=True,
             )
-            if n % 2 == 0:
-                nc.scalar.activation(scores[:, cols], bank[:], COPY)
-            else:
-                nc.vector.tensor_copy(out=scores[:, cols], in_=bank[:])
+            nc.vector.tensor_copy(out=scores[:, cols], in_=bank[:])
 
         first = slice(0, LIST_COLS // 2)
         second = slice(LIST_COLS // 2, LIST_COLS)
@@ -98,20 +99,19 @@ def tile_attend_pairproduct_lean_timesold_heads_kernel(
         old_a = pool.tile([P, HALF], F32, name="old_a")
         nc.scalar.activation(old_a[:], old_sb[:].indirect(list3[:, first]), COPY)
         left_a = pool.tile([P, HALF], F32, name="left_a")
-        nc.scalar.activation(left_a[:], scores[:].indirect(list1[:, first]), COPY)
-        right_a = pool.tile([P, HALF], F32, name="right_a")
+        nc.vector.tensor_copy(left_a[:], scores[:].indirect(list1[:, first]))
+        right_a = pool.tile([P, HALF], F32, name="right_a", tag="right")
         nc.vector.tensor_tensor(right_a[:], scores[:].indirect(list2[:, first]), old_a[:], MULT)
         nc.vector.tensor_tensor(placed[:].indirect(list4[:, first]), left_a[:], right_a[:], MULT)
 
         old_b = pool.tile([P, HALF], F32, name="old_b")
         nc.scalar.activation(old_b[:], old_sb[:].indirect(list3[:, second]), COPY)
-        mid_b = pool.tile([P, HALF], F32, name="mid_b")
-        nc.scalar.activation(mid_b[:], scores[:].indirect(list2[:, second]), COPY)
-        left_b = pool.tile([P, HALF], F32, name="left_b")
-        nc.scalar.activation(left_b[:], scores[:].indirect(list1[:, second]), COPY)
-        right_b = pool.tile([P, HALF], F32, name="right_b")
-        nc.vector.tensor_tensor(right_b[:], mid_b[:], old_b[:], MULT)
-        nc.vector.tensor_tensor(placed[:].indirect(list4[:, second]), left_b[:], right_b[:], MULT)
+        pair_b = pool.tile([P, 2, HALF], F32, name="pair_b", tag="old_then_second")
+        nc.scalar.activation(pair_b[:, 0, :], scores[:].indirect(list2[:, second]), COPY)
+        nc.scalar.activation(pair_b[:, 1, :], scores[:].indirect(list1[:, second]), COPY)
+        right_b = pool.tile([P, HALF], F32, name="right_b", tag="right")
+        nc.vector.tensor_tensor(right_b[:], pair_b[:, 0, :], old_b[:], MULT)
+        nc.vector.tensor_tensor(placed[:].indirect(list4[:, second]), pair_b[:, 1, :], right_b[:], MULT)
 
         for s in range(T // STORE_COLS):
             cols = slice(s * STORE_COLS, (s + 1) * STORE_COLS)

@@ -20,10 +20,11 @@ P = 128
 PACK = 4
 LIST_COLS = SLOTS // 16
 KEY_LOADS = 2
-N_TILE = 256
+PASS_WIDTHS = (256, 256, 256, 128, 128)
+SCALAR_BANKS = (0, 2)
 HALF = SLOTS // 2
 STORE_COLS = 256
-Q_SPLIT = 88
+Q_SPLIT = 22
 
 
 def tile_attend_pairproduct_lean_timesold_heads_kernel(
@@ -65,9 +66,10 @@ def tile_attend_pairproduct_lean_timesold_heads_kernel(
         nc.vector.memset(placed[:], 0.0)
 
         q_bf = pool.tile([P, Q, PACK], BF16, name="q_bf", align_bytes=64)
-        q_view = q_raw[:].rearrange("p j q -> p q j")
-        nc.vector.tensor_copy(out=q_bf[:, :Q_SPLIT, :], in_=q_view[:, :Q_SPLIT, :])
-        nc.scalar.activation(q_bf[:, Q_SPLIT:, :], q_view[:, Q_SPLIT:, :], COPY)
+        q_src = q_raw[:].rearrange("p j (c i) -> p c j i", i=4)
+        q_dst = q_bf[:].rearrange("p (c i) j -> p c j i", i=4)
+        nc.vector.tensor_copy(out=q_dst[:, :Q_SPLIT], in_=q_src[:, :Q_SPLIT])
+        nc.scalar.activation(q_dst[:, Q_SPLIT:], q_src[:, Q_SPLIT:], COPY)
         q_codes = pool.tile([P, Q], U32, name="q_codes", align_bytes=64)
         q_scales = pool.tile([P, Q], U8, name="q_scales", align_bytes=64)
         nc.vector.quantize_mx(
@@ -78,40 +80,43 @@ def tile_attend_pairproduct_lean_timesold_heads_kernel(
         nc.sync.dma_start(out=base_sb[:], in_=base)
 
         scores = pool.tile([P, T], F32, name="scores")
-        for n in range(T // N_TILE):
-            cols = slice(n * N_TILE, (n + 1) * N_TILE)
-            h, c0 = divmod(n * N_TILE, load_cols)
-            bank = psum.tile([P, N_TILE], F32, name="bank%d" % n)
+        c0 = 0
+        for n, width in enumerate(PASS_WIDTHS):
+            cols = slice(c0, c0 + width)
+            h, h0 = divmod(c0, load_cols)
+            bank = psum.tile([P, width], F32, name="bank%d" % n)
             nc.tensor.matmul_mx(
                 out=bank[:],
                 lhsT=q_codes[:].bitcast(FP8X4),
                 lhsT_scale=q_scales[:],
-                rhs=key_words[h][:, c0 : c0 + N_TILE].bitcast(FP8X4),
+                rhs=key_words[h][:, h0 : h0 + width].bitcast(FP8X4),
                 rhs_scale=key_scales[:, cols],
                 start=True,
                 stop=True,
             )
-            nc.vector.tensor_copy(out=scores[:, cols], in_=bank[:])
+            if n in SCALAR_BANKS:
+                nc.scalar.activation(scores[:, cols], bank[:], COPY)
+            else:
+                nc.vector.tensor_copy(out=scores[:, cols], in_=bank[:])
+            c0 = c0 + width
 
-        first = slice(0, LIST_COLS // 2)
-        second = slice(LIST_COLS // 2, LIST_COLS)
+        def entries(lst, start, stop):
+            return lst[:, start // 16 : stop // 16]
 
-        old_a = pool.tile([P, HALF], F32, name="old_a")
-        nc.scalar.activation(old_a[:], old_sb[:].indirect(list3[:, first]), COPY)
-        left_a = pool.tile([P, HALF], F32, name="left_a")
-        nc.vector.tensor_copy(left_a[:], scores[:].indirect(list1[:, first]))
-        right_a = pool.tile([P, HALF], F32, name="right_a", tag="right")
-        nc.vector.tensor_tensor(right_a[:], scores[:].indirect(list2[:, first]), old_a[:], MULT)
-        nc.vector.tensor_tensor(placed[:].indirect(list4[:, first]), left_a[:], right_a[:], MULT)
-
-        old_b = pool.tile([P, HALF], F32, name="old_b")
-        nc.scalar.activation(old_b[:], old_sb[:].indirect(list3[:, second]), COPY)
-        pair_b = pool.tile([P, 2, HALF], F32, name="pair_b", tag="old_then_second")
-        nc.scalar.activation(pair_b[:, 0, :], scores[:].indirect(list2[:, second]), COPY)
-        nc.scalar.activation(pair_b[:, 1, :], scores[:].indirect(list1[:, second]), COPY)
-        right_b = pool.tile([P, HALF], F32, name="right_b", tag="right")
-        nc.vector.tensor_tensor(right_b[:], pair_b[:, 0, :], old_b[:], MULT)
-        nc.vector.tensor_tensor(placed[:].indirect(list4[:, second]), pair_b[:, 1, :], right_b[:], MULT)
+        picked_old = pool.tile([P, SLOTS], F32, name="picked_old")
+        nc.vector.tensor_copy(picked_old[:, :HALF], old_sb[:].indirect(entries(list3, 0, HALF)))
+        nc.scalar.activation(picked_old[:, HALF:], old_sb[:].indirect(entries(list3, HALF, SLOTS)), COPY)
+        left = pool.tile([P, SLOTS], F32, name="left", tag="old_then_second")
+        nc.scalar.activation(left[:], scores[:].indirect(list1[:]), COPY)
+        right = pool.tile([P, SLOTS], F32, name="right")
+        for s0 in (HALF, 0):
+            nc.vector.tensor_tensor(
+                right[:, s0 : s0 + HALF],
+                scores[:].indirect(entries(list2, s0, s0 + HALF)),
+                picked_old[:, s0 : s0 + HALF],
+                MULT,
+            )
+        nc.vector.tensor_tensor(placed[:].indirect(list4[:]), left[:], right[:], MULT)
 
         for s in range(T // STORE_COLS):
             cols = slice(s * STORE_COLS, (s + 1) * STORE_COLS)

@@ -24,6 +24,7 @@ PASS_WIDTHS = (256, 256, 256, 128, 128)
 SCALAR_BANKS = (0, 2)
 HALF = SLOTS // 2
 STORE_COLS = 256
+PLANE_COLS = 256
 Q_SPLIT = 22
 
 
@@ -35,14 +36,16 @@ def tile_attend_pairproduct_lean_timesold_heads_kernel(
         pool = ctx.enter_context(tc.tile_pool(name="held", bufs=1))
         psum = ctx.enter_context(tc.psum_pool(name="psum", bufs=1))
 
-        key_scales = pool.tile([P, T], U8, name="key_scales", align_bytes=64)
+        key_scales = pool.tile([P, PLANE_COLS], U8, name="key_scales", align_bytes=64)
+        nc.vector.memset(key_scales[:].bitcast(I32), 0)
+        staged_scales = pool.tile([P, PLANE_COLS], U8, name="staged_scales")
         q_raw = pool.tile([P, PACK, Q], F32, name="q_raw", tag="q_then_base")
         nc.sync.dma_start(out=q_raw[:], in_=query.rearrange("(p j) q -> p j q", j=PACK))
         for quad in range(4):
             rows = keys_scales[0, 4 * quad : 4 * quad + 4, :].bitcast(I32)
             nc.sync.dma_start(
-                out=key_scales[32 * quad : 32 * quad + 32, :].bitcast(I32),
-                in_=rows.unsqueeze(0).broadcast_to([8, 4, T // 4]),
+                out=staged_scales[32 * quad : 32 * quad + 16, :].bitcast(I32),
+                in_=rows.rearrange("r (n c) -> n r c", n=4),
             )
         words_i32 = keys_words[0].rearrange("p t r -> p (t r)").bitcast(I32)
         load_cols = T // KEY_LOADS
@@ -70,6 +73,9 @@ def tile_attend_pairproduct_lean_timesold_heads_kernel(
         q_dst = q_bf[:].rearrange("p (c i) j -> p c j i", i=4)
         nc.vector.tensor_copy(out=q_dst[:, :Q_SPLIT], in_=q_src[:, :Q_SPLIT])
         nc.scalar.activation(q_dst[:, Q_SPLIT:], q_src[:, Q_SPLIT:], COPY)
+        for quad in range(4):
+            live = slice(32 * quad, 32 * quad + 16)
+            nc.scalar.copy(key_scales[live, :].bitcast(U32), staged_scales[live, :].bitcast(U32))
         q_codes = pool.tile([P, Q], U32, name="q_codes", align_bytes=64)
         q_scales = pool.tile([P, Q], U8, name="q_scales", align_bytes=64)
         nc.vector.quantize_mx(
@@ -84,13 +90,14 @@ def tile_attend_pairproduct_lean_timesold_heads_kernel(
         for n, width in enumerate(PASS_WIDTHS):
             cols = slice(c0, c0 + width)
             h, h0 = divmod(c0, load_cols)
+            plane, p0 = divmod(c0, PLANE_COLS)
             bank = psum.tile([P, width], F32, name="bank%d" % n)
             nc.tensor.matmul_mx(
                 out=bank[:],
                 lhsT=q_codes[:].bitcast(FP8X4),
                 lhsT_scale=q_scales[:],
                 rhs=key_words[h][:, h0 : h0 + width].bitcast(FP8X4),
-                rhs_scale=key_scales[:, cols],
+                rhs_scale=key_scales[4 * plane :, p0 : p0 + width],
                 start=True,
                 stop=True,
             )

from contextlib import ExitStack

import concourse.mybir as mybir

D, T, SLOTS, Q = 512, 1024, 512, 128
FLOPS = 2 * D * T * Q

F32 = mybir.dt.float32
BF16 = mybir.dt.bfloat16
I32 = mybir.dt.int32
U32 = mybir.dt.uint32
U16 = mybir.dt.uint16
U8 = mybir.dt.uint8
FP8X4 = mybir.dt.float8_e4m3fn_x4
MULT = mybir.AluOpType.mult
ADD = mybir.AluOpType.add
COPY = mybir.ActivationFunctionType.Copy

P = 128
PACK = 4
LIST_COLS = SLOTS // 16
KEY_LOADS = 2
PASS_WIDTHS = (256, 256, 256, 128, 128)
SCALAR_BANKS = (0, 2)
HALF = SLOTS // 2
STORE_COLS = 256
PLANE_COLS = 256
Q_SPLIT = 22


def tile_attend_pairproduct_lean_timesold_heads_kernel(
    tc, query, keys_words, keys_scales, old, base, offs, offs2, offs3, offs4, out
):
    nc = tc.nc
    with ExitStack() as ctx:
        pool = ctx.enter_context(tc.tile_pool(name="held", bufs=1))
        psum = ctx.enter_context(tc.psum_pool(name="psum", bufs=1))

        key_scales = pool.tile([P, PLANE_COLS], U8, name="key_scales", align_bytes=64)
        nc.vector.memset(key_scales[:].bitcast(I32), 0)
        staged_scales = pool.tile([P, PLANE_COLS], U8, name="staged_scales")
        q_raw = pool.tile([P, PACK, Q], F32, name="q_raw", tag="q_then_base")
        nc.sync.dma_start(out=q_raw[:], in_=query.rearrange("(p j) q -> p j q", j=PACK))
        for quad in range(4):
            rows = keys_scales[0, 4 * quad : 4 * quad + 4, :].bitcast(I32)
            nc.sync.dma_start(
                out=staged_scales[32 * quad : 32 * quad + 16, :].bitcast(I32),
                in_=rows.rearrange("r (n c) -> n r c", n=4),
            )
        words_i32 = keys_words[0].rearrange("p t r -> p (t r)").bitcast(I32)
        load_cols = T // KEY_LOADS
        key_words = []
        for h in range(KEY_LOADS):
            part = pool.tile([P, load_cols], U32, name="key_words%d" % h, align_bytes=64)
            nc.sync.dma_start(out=part[:].bitcast(I32), in_=words_i32[:, h * load_cols : (h + 1) * load_cols])
            key_words.append(part)
        old_sb = pool.tile([P, T], F32, name="old_sb", tag="old_then_second")
        nc.sync.dma_start(out=old_sb[:], in_=old)
        list3 = pool.tile([P, LIST_COLS], U16, name="list3")
        nc.sync.dma_start(list3[:], offs3)
        list1 = pool.tile([P, LIST_COLS], U16, name="list1")
        nc.sync.dma_start(list1[:], offs)
        list2 = pool.tile([P, LIST_COLS], U16, name="list2")
        nc.sync.dma_start(list2[:], offs2)
        list4 = pool.tile([P, LIST_COLS], U16, name="list4")
        nc.sync.dma_start(list4[:], offs4)

        placed = pool.tile([P, T], F32, name="placed")
        nc.vector.memset(placed[:], 0.0)

        q_bf = pool.tile([P, Q, PACK], BF16, name="q_bf", align_bytes=64)
        q_src = q_raw[:].rearrange("p j (c i) -> p c j i", i=4)
        q_dst = q_bf[:].rearrange("p (c i) j -> p c j i", i=4)
        nc.vector.tensor_copy(out=q_dst[:, :Q_SPLIT], in_=q_src[:, :Q_SPLIT])
        nc.scalar.activation(q_dst[:, Q_SPLIT:], q_src[:, Q_SPLIT:], COPY)
        for quad in range(4):
            live = slice(32 * quad, 32 * quad + 16)
            nc.scalar.copy(key_scales[live, :].bitcast(U32), staged_scales[live, :].bitcast(U32))
        q_codes = pool.tile([P, Q], U32, name="q_codes", align_bytes=64)
        q_scales = pool.tile([P, Q], U8, name="q_scales", align_bytes=64)
        nc.vector.quantize_mx(
            out=q_codes[:].bitcast(FP8X4), scales=q_scales[:], in_=q_bf[:].rearrange("p q j -> p (q j)")
        )

        base_sb = pool.tile([P, T], F32, name="base_sb", tag="q_then_base")
        nc.sync.dma_start(out=base_sb[:], in_=base)

        scores = pool.tile([P, T], F32, name="scores")
        c0 = 0
        for n, width in enumerate(PASS_WIDTHS):
            cols = slice(c0, c0 + width)
            h, h0 = divmod(c0, load_cols)
            plane, p0 = divmod(c0, PLANE_COLS)
            bank = psum.tile([P, width], F32, name="bank%d" % n)
            nc.tensor.matmul_mx(
                out=bank[:],
                lhsT=q_codes[:].bitcast(FP8X4),
                lhsT_scale=q_scales[:],
                rhs=key_words[h][:, h0 : h0 + width].bitcast(FP8X4),
                rhs_scale=key_scales[4 * plane :, p0 : p0 + width],
                start=True,
                stop=True,
            )
            if n in SCALAR_BANKS:
                nc.scalar.activation(scores[:, cols], bank[:], COPY)
            else:
                nc.vector.tensor_copy(out=scores[:, cols], in_=bank[:])
            c0 = c0 + width

        def entries(lst, start, stop):
            return lst[:, start // 16 : stop // 16]

        picked_old = pool.tile([P, SLOTS], F32, name="picked_old")
        nc.vector.tensor_copy(picked_old[:, :HALF], old_sb[:].indirect(entries(list3, 0, HALF)))
        nc.scalar.activation(picked_old[:, HALF:], old_sb[:].indirect(entries(list3, HALF, SLOTS)), COPY)
        left = pool.tile([P, SLOTS], F32, name="left", tag="old_then_second")
        nc.scalar.activation(left[:], scores[:].indirect(list1[:]), COPY)
        right = pool.tile([P, SLOTS], F32, name="right")
        for s0 in (HALF, 0):
            nc.vector.tensor_tensor(
                right[:, s0 : s0 + HALF],
                scores[:].indirect(entries(list2, s0, s0 + HALF)),
                picked_old[:, s0 : s0 + HALF],
                MULT,
            )
        nc.vector.tensor_tensor(placed[:].indirect(list4[:]), left[:], right[:], MULT)

        for s in range(T // STORE_COLS):
            cols = slice(s * STORE_COLS, (s + 1) * STORE_COLS)
            result = pool.tile([P, STORE_COLS], F32, name="result%d" % s)
            nc.vector.tensor_tensor(result[:], placed[:, cols], base_sb[:, cols], ADD)
            queue = nc.sync if s % 2 == 0 else nc.scalar
            queue.dma_start(out=out[:, cols], in_=result[:])
